import numpy as np
import ml_dtypes


def mxq(x, axis, fmt="e4m3"):
    dtype, down = {"e4m3": (ml_dtypes.float8_e4m3fn, 7), "e5m2": (ml_dtypes.float8_e5m2, 14)}[fmt]
    v = np.moveaxis(np.asarray(x, np.float32).astype(ml_dtypes.bfloat16).astype(np.float64), axis, -1)
    blocks = v.reshape(v.shape[:-1] + (-1, 32))
    amax = np.abs(blocks).max(-1, keepdims=True)
    byte = np.maximum(np.where(amax > 0, np.frexp(amax)[1] - 1 + 127, 0) - down, 1)
    scale = np.exp2(byte - 127.0)
    codes = (blocks / scale).astype(np.float32).astype(dtype).astype(np.float64)
    return np.moveaxis((codes * scale).reshape(v.shape), -1, axis)


WIDE = False


def mx_kscale(k):
    if not WIDE:
        return np.ones(k)
    levels = np.array([10, -10, 5, -5, 0])
    if k % 512:
        return np.exp2(np.random.permutation(np.resize(levels, k // 32))).repeat(32)
    a = np.empty((k // 512, 16))
    for p in range(k // 512):
        a[p, :8] = np.random.permutation(np.resize(levels, 8))
        for g in range(8):
            far = levels[np.abs(levels - a[p, g]) >= 10]
            a[p, g + 8] = far[np.random.randint(len(far))]
    return np.exp2(a.ravel()).repeat(32)


def f64(x):
    return np.asarray(x).astype(np.float64)


def striped(idx):
    return np.tile(idx.reshape(-1, 16).T, (8, 1)).astype(np.uint16)


def unstriped(offs):
    return offs[:16].T.reshape(-1).astype(np.int64)


def relu(v):
    return np.maximum(v, 0.0)


K, T, E, C, N = 1024, 768, 4, 128, 1024
M = 512


def by_expert(wq, xq):
    return np.concatenate([wq[e].T @ xq[:, e * C:(e + 1) * C] for e in range(E)], axis=1)


def setup_inputs():
    n = np.random.standard_normal
    s = mx_kscale(K)[:, None]
    v = mx_kscale(N)
    return {
        "xT": (n((K, T)) * s).astype(np.float32),
        "w": (n((E, K, N)) / np.sqrt(K) / s[None] * v[None, None, :]).astype(np.float32),
        "b": (0.3 * n((N, E)) * v[:, None]).astype(np.float32),
        "wp": (n((N, M)) / np.sqrt(N) / v[:, None]).astype(np.float32),
        "gate": np.tile(np.random.uniform(0.2, 1.0, E * C), (N, 1)).astype(np.float32),
        "offs": striped(np.random.permutation(T)[:E * C]),
    }


def reference(xT, w, b, wp, gate, offs):
    idx = unstriped(offs)
    xq = mxq(f64(xT)[:, idx], 0, "e4m3")
    y = by_expert(mxq(f64(w), 1, "e4m3"), xq)
    y = relu(y + np.repeat(f64(b), C, axis=1))
    c = np.zeros((N, T))
    c[:, idx] = f64(gate) * y
    return mxq(f64(wp), 0, "e4m3").T @ mxq(c, 0, "e4m3")

@@ -1,0 +1,246 @@
+from contextlib import ExitStack
+
+import concourse.mybir as mybir
+
+F32 = mybir.dt.float32
+BF16 = mybir.dt.bfloat16
+U32 = mybir.dt.uint32
+U16 = mybir.dt.uint16
+U8 = mybir.dt.uint8
+FP8X4 = mybir.dt.float8_e4m3fn_x4
+COPY = mybir.ActivationFunctionType.Copy
+RELU = mybir.ActivationFunctionType.Relu
+MULT = mybir.AluOpType.mult
+
+P = 128
+K, T, E, C, N, M = 1024, 768, 4, 128, 1024, 512
+PASS = 512
+PASSES = K // PASS
+SLOTS = E * C
+
+FLOPS = 2 * SLOTS * K * N + 2 * SLOTS * N * M
+BYTES = 4 * (K * T + E * K * N + N * E + N * M + SLOTS + M * T) + 2 * P * (SLOTS // 16)
+
+RAW_BUFS = 6
+LAG = 2
+S_COLS = 92
+
+
+def tile_moe_nxt_lin_relu_kernel(tc, xT, w, b, wp, gate, offs, out):
+    nc = tc.nc
+    with ExitStack() as ctx:
+        keep = ctx.enter_context(tc.tile_pool(name="keep", bufs=1))
+        rawp = ctx.enter_context(tc.tile_pool(name="rawp", bufs=RAW_BUFS))
+        stage = ctx.enter_context(tc.tile_pool(name="stage", bufs=4))
+        psum = ctx.enter_context(tc.psum_pool(name="psum", bufs=3))
+
+        offsets = keep.tile([P, SLOTS // 16], U16, name="offsets")
+        nc.sync.dma_start(offsets[:], offs)
+
+        bias = keep.tile([P, 2, 16], F32, name="bias")
+        gates = keep.tile([P, SLOTS], F32, name="gates")
+
+        x_codes = [keep.tile([P, T], U32, name=f"x_codes{i}", align_bytes=64) for i in range(PASSES)]
+        x_scales = [keep.tile([P, T], U8, name=f"x_scales{i}", align_bytes=64) for i in range(PASSES)]
+        g_codes = [keep.tile([P, SLOTS], U32, name=f"g_codes{i}", align_bytes=64) for i in range(PASSES)]
+        g_scales = [keep.tile([P, SLOTS], U8, name=f"g_scales{i}", align_bytes=64) for i in range(PASSES)]
+        wp_codes = [keep.tile([P, M], U32, name=f"wp_codes{i}", align_bytes=64) for i in range(PASSES)]
+        wp_scales = [keep.tile([P, M], U8, name=f"wp_scales{i}", align_bytes=64) for i in range(PASSES)]
+        outs = [keep.tile([P, T], F32, name=f"outs{i}") for i in range(M // P)]
+        for t in x_scales:
+            nc.gpsimd.memset(t[:], 0)
+        for t in outs:
+            nc.gpsimd.memset(t[:], 0.0)
+
+        w_codes = {}
+        w_scales = {}
+
+        loads = []
+
+        def load(src, width):
+            def go():
+                raw = rawp.tile([P, 4, width], F32, name="raw")
+                nc.sync.dma_start(raw[:], src.rearrange("(p j) c -> p j c", j=4))
+                return raw
+            loads.append(go)
+            return len(loads) - 1
+
+        def load_small():
+            nc.sync.dma_start(gates[:], gate[0:P, :])
+            nc.sync.dma_start(bias[:].rearrange("p a (r e) -> p a r e", r=4), b.rearrange("(a q r) e -> q a r e", a=2, r=4))
+
+        steps = []
+        for i in range(PASSES):
+            for c0, c1 in ((0, 256), (256, 768)) if i == 0 else ((0, 512), (512, 768)):
+                steps.append((load(xT[i * PASS:(i + 1) * PASS, c0:c1], c1 - c0), 0, "x", i, c0, c1 - c0))
+        small_after = len(loads)
+        for e in range(E):
+            if e < E - 1:
+                for i in range(PASSES):
+                    l = load(w[e, i * PASS:(i + 1) * PASS, :], N)
+                    for a in range(2):
+                        steps.append((l, a * PASS, "w", i, e, a))
+                    if e == 0 and i == 0:
+                        for a in range(PASSES):
+                            l = load(wp[a * PASS:(a + 1) * PASS, :], M)
+                            steps.append((l, 0, "wp", a, 0, M))
+            else:
+                for a in range(2):
+                    for i in range(PASSES):
+                        l = load(w[e, i * PASS:(i + 1) * PASS, a * PASS:(a + 1) * PASS], PASS)
+                        steps.append((l, 0, "w", i, e, a))
+
+        raws = {}
+        issued = [0]
+
+        def issue_to(n):
+            while issued[0] < min(n, len(loads)):
+                if issued[0] == small_after:
+                    load_small()
+                raws[issued[0]] = loads[issued[0]]()
+                issued[0] += 1
+
+        def split_copy(dst, src, groups):
+            cut = groups * S_COLS // 128 // 4 * 4
+            nc.scalar.activation(dst[:, :cut], src[:, :cut], COPY)
+            nc.vector.tensor_copy(dst[:, cut:], src[:, cut:])
+
+        def interleave(step):
+            l, c0, kind, i, u, v = step
+            raw = raws[l]
+            if kind == "w":
+                grouped = stage.tile([P, 2048], BF16, name="grouped_w", align_bytes=64)
+                dst = grouped[:].rearrange("p (r m j) -> p m j r", r=4, j=4)
+                src = raw[:, :, c0:c0 + PASS].rearrange("p j (m r) -> p m j r", r=4)
+                split_copy(dst, src, 128)
+            else:
+                width = v
+                grouped = stage.tile([P, 4 * width], BF16, name="grouped_x", align_bytes=64)
+                dst = grouped[:].rearrange("p (g c j) -> p g j c", c=4, j=4)
+                src = raw[:, :, :].rearrange("p j (g c) -> p g j c", c=4)
+                split_copy(dst, src, width // 4)
+            return grouped
+
+        def quantise(step, grouped):
+            l, c0, kind, i, u, v = step
+            if kind == "x":
+                codes, scales = x_codes[i][:, u:u + v], x_scales[i][:, u:u + v]
+            elif kind == "wp":
+                codes, scales = wp_codes[i][:], wp_scales[i][:]
+            else:
+                ct = keep.tile([P, PASS], U32, name=f"w_codes_{u}_{i}_{v}", align_bytes=64)
+                st = keep.tile([P, PASS], U8, name=f"w_scales_{u}_{i}_{v}", align_bytes=64)
+                w_codes[u, i, v], w_scales[u, i, v] = ct, st
+                codes, scales = ct[:], st[:]
+            nc.vector.quantize_mx(out=codes.bitcast(FP8X4), scales=scales, in_=grouped[:])
+
+        def gather(i):
+            nc.vector.tensor_copy(g_codes[i][:], x_codes[i][:].indirect(offsets[:]))
+            nc.vector.tensor_copy(g_scales[i][:], x_scales[i][:].indirect(offsets[:]))
+
+        def experts(e, a):
+            cols = slice(e * C, (e + 1) * C)
+            acc = psum.tile([P, 4, C], F32, name="acc_y")
+            for r in range(4):
+                rows = slice(r * P, (r + 1) * P)
+                for i in range(PASSES):
+                    nc.tensor.matmul_mx(
+                        out=acc[:, r, :],
+                        lhsT=w_codes[e, i, a][:, rows].bitcast(FP8X4), lhsT_scale=w_scales[e, i, a][:, rows],
+                        rhs=g_codes[i][:, cols].bitcast(FP8X4), rhs_scale=g_scales[i][:, cols],
+                        start=(i == 0), stop=(i == PASSES - 1),
+                    )
+            return acc
+
+        def activate(e, a, acc):
+            y = stage.tile([P, 4, C], F32, name="y")
+            for r in range(4):
+                nc.scalar.activation(y[:, r, :], acc[:, r, :], RELU, bias=bias[:, a, 4 * r + e:4 * r + e + 1])
+            return y
+
+        def weigh(e, y):
+            c = stage.tile([P, C, 4], BF16, name="c", align_bytes=64)
+            g = gates[:, e * C:(e + 1) * C].unsqueeze(2).to_broadcast([P, C, 4])
+            nc.vector.tensor_tensor(c[:], y[:].rearrange("p r s -> p s r"), g, MULT)
+            return c
+
+        def quantise_c(c):
+            codes = stage.tile([P, C], U32, name="c_codes", align_bytes=64)
+            scales = stage.tile([P, C], U8, name="c_scales", align_bytes=64)
+            nc.vector.quantize_mx(out=codes[:].bitcast(FP8X4), scales=scales[:], in_=c[:].rearrange("p s r -> p (s r)"))
+            return codes, scales
+
+        def project(halves):
+            acc = psum.tile([P, 4, C], F32, name="acc_z")
+            for f in range(M // P):
+                rows = slice(f * P, (f + 1) * P)
+                for a in range(2):
+                    codes, scales = halves[a]
+                    nc.tensor.matmul_mx(
+                        out=acc[:, f, :],
+                        lhsT=wp_codes[a][:, rows].bitcast(FP8X4), lhsT_scale=wp_scales[a][:, rows],
+                        rhs=codes[:].bitcast(FP8X4), rhs_scale=scales[:],
+                        start=(a == 0), stop=(a == 1),
+                    )
+            return acc
+
+        def fetch(acc):
+            z = stage.tile([P, 4, C], F32, name="z")
+            nc.scalar.activation(z[:], acc[:], COPY)
+            return z
+
+        def scatter(e, z, f):
+            nc.vector.tensor_copy(outs[f][:].indirect(offsets[:, e * (C // 16):(e + 1) * (C // 16)]), z[:, f, :])
+            if e == E - 1:
+                nc.sync.dma_start(out[f * P:(f + 1) * P, :], outs[f][:])
+
+        due = {}
+
+        def at(n, fn):
+            due.setdefault(n, []).append(fn)
+
+        halves = {}
+
+        def stage_experts(n, e, a):
+            acc = experts(e, a)
+            at(n + 1, lambda: stage_activate(n + 1, e, a, acc))
+
+        def stage_activate(n, e, a, acc):
+            y = activate(e, a, acc)
+            at(n + 1, lambda: stage_weigh(n + 1, e, a, y))
+
+        def stage_weigh(n, e, a, y):
+            c = weigh(e, y)
+            at(n + 1, lambda: stage_c(n + 1, e, a, c))
+
+        def stage_c(n, e, a, c):
+            halves[e, a] = quantise_c(c)
+            if a == 1:
+                acc = project([halves[e, 0], halves[e, 1]])
+                at(n + 1, lambda: stage_fetch(n + 1, e, acc))
+
+        def stage_fetch(n, e, acc):
+            z = fetch(acc)
+            for f in range(M // P):
+                at(n + 1 + f, lambda f=f: scatter(e, z, f))
+
+        def after_quantise(n, step):
+            l, c0, kind, i, u, v = step
+            if kind == "x" and u + v == T:
+                at(n + 1, lambda: gather(i))
+            if kind == "w" and i == PASSES - 1:
+                stage_experts(n, u, v)
+
+        waiting = []
+        n = 0
+        while n < len(steps) or waiting or any(k >= n for k in due):
+            if waiting and (len(waiting) == LAG or n >= len(steps)):
+                step, grouped = waiting.pop(0)
+                quantise(step, grouped)
+                after_quantise(n, step)
+            if n < len(steps):
+                issue_to(steps[n][0] + RAW_BUFS)
+                waiting.append((steps[n], interleave(steps[n])))
+            for fn in due.get(n, []):
+                fn()
+            n += 1

@@ -21,9 +21,11 @@ SLOTS = E * C
 FLOPS = 2 * SLOTS * K * N + 2 * SLOTS * N * M
 BYTES = 4 * (K * T + E * K * N + N * E + N * M + SLOTS + M * T) + 2 * P * (SLOTS // 16)
 
-RAW_BUFS = 6
-LAG = 2
-S_COLS = 92
+RAW_BUFS = 10
+LAG = 1
+ZL = (1, "post")
+SC = ((1, "late"), (2, "late"), (3, "late"), (4, "late"))
+S_EARLY, S_MID, S_LAST = 64, 88, 56
 
 
 def tile_moe_nxt_lin_relu_kernel(tc, xT, w, b, wp, gate, offs, out):
@@ -74,21 +76,14 @@ def tile_moe_nxt_lin_relu_kernel(tc, xT, w, b, wp, gate, offs, out):
             for c0, c1 in ((0, 256), (256, 768)) if i == 0 else ((0, 512), (512, 768)):
                 steps.append((load(xT[i * PASS:(i + 1) * PASS, c0:c1], c1 - c0), 0, "x", i, c0, c1 - c0))
         small_after = len(loads)
+        for i in range(PASSES):
+            l = load(wp[i * PASS:(i + 1) * PASS, :], M)
+            steps.append((l, 0, "wp", i, 0, M))
         for e in range(E):
-            if e < E - 1:
+            for a in range(2):
                 for i in range(PASSES):
-                    l = load(w[e, i * PASS:(i + 1) * PASS, :], N)
-                    for a in range(2):
-                        steps.append((l, a * PASS, "w", i, e, a))
-                    if e == 0 and i == 0:
-                        for a in range(PASSES):
-                            l = load(wp[a * PASS:(a + 1) * PASS, :], M)
-                            steps.append((l, 0, "wp", a, 0, M))
-            else:
-                for a in range(2):
-                    for i in range(PASSES):
-                        l = load(w[e, i * PASS:(i + 1) * PASS, a * PASS:(a + 1) * PASS], PASS)
-                        steps.append((l, 0, "w", i, e, a))
+                    l = load(w[e, i * PASS:(i + 1) * PASS, a * PASS:(a + 1) * PASS], PASS)
+                    steps.append((l, 0, "w", i, e, a))
 
         raws = {}
         issued = [0]
@@ -100,25 +95,28 @@ def tile_moe_nxt_lin_relu_kernel(tc, xT, w, b, wp, gate, offs, out):
                 raws[issued[0]] = loads[issued[0]]()
                 issued[0] += 1
 
-        def split_copy(dst, src, groups):
-            cut = groups * S_COLS // 128 // 4 * 4
+        def split_copy(dst, src, groups, sc):
+            cut = groups * sc // 128 // 4 * 4
             nc.scalar.activation(dst[:, :cut], src[:, :cut], COPY)
             nc.vector.tensor_copy(dst[:, cut:], src[:, cut:])
 
-        def interleave(step):
+        def share(n):
+            return S_EARLY if n < 10 else S_LAST if n >= len(steps) - 1 else S_MID
+
+        def interleave(step, sc):
             l, c0, kind, i, u, v = step
             raw = raws[l]
             if kind == "w":
                 grouped = stage.tile([P, 2048], BF16, name="grouped_w", align_bytes=64)
                 dst = grouped[:].rearrange("p (r m j) -> p m j r", r=4, j=4)
                 src = raw[:, :, c0:c0 + PASS].rearrange("p j (m r) -> p m j r", r=4)
-                split_copy(dst, src, 128)
+                split_copy(dst, src, 128, sc)
             else:
                 width = v
                 grouped = stage.tile([P, 4 * width], BF16, name="grouped_x", align_bytes=64)
                 dst = grouped[:].rearrange("p (g c j) -> p g j c", c=4, j=4)
                 src = raw[:, :, :].rearrange("p j (g c) -> p g j c", c=4)
-                split_copy(dst, src, width // 4)
+                split_copy(dst, src, width // 4, sc)
             return grouped
 
         def quantise(step, grouped):
@@ -196,51 +194,55 @@ def tile_moe_nxt_lin_relu_kernel(tc, xT, w, b, wp, gate, offs, out):
 
         due = {}
 
-        def at(n, fn):
-            due.setdefault(n, []).append(fn)
+        def at(n, where, fn):
+            due.setdefault((n, where), []).append(fn)
+
+        def run(n, where):
+            for fn in due.get((n, where), []):
+                fn()
 
         halves = {}
 
         def stage_experts(n, e, a):
             acc = experts(e, a)
-            at(n + 1, lambda: stage_activate(n + 1, e, a, acc))
+            at(n, "post", lambda: stage_activate(n, e, a, acc))
 
         def stage_activate(n, e, a, acc):
             y = activate(e, a, acc)
-            at(n + 1, lambda: stage_weigh(n + 1, e, a, y))
+            at(n + 1, "pre", lambda: stage_weigh(n + 1, e, a, y))
 
         def stage_weigh(n, e, a, y):
             c = weigh(e, y)
-            at(n + 1, lambda: stage_c(n + 1, e, a, c))
+            at(n, "post", lambda: stage_c(n, e, a, c))
 
         def stage_c(n, e, a, c):
             halves[e, a] = quantise_c(c)
             if a == 1:
                 acc = project([halves[e, 0], halves[e, 1]])
-                at(n + 1, lambda: stage_fetch(n + 1, e, acc))
+                at(n + ZL[0], ZL[1], lambda: stage_fetch(n + ZL[0], e, acc))
 
         def stage_fetch(n, e, acc):
             z = fetch(acc)
             for f in range(M // P):
-                at(n + 1 + f, lambda f=f: scatter(e, z, f))
+                at(n + SC[f][0], SC[f][1], lambda f=f: scatter(e, z, f))
 
         def after_quantise(n, step):
             l, c0, kind, i, u, v = step
             if kind == "x" and u + v == T:
-                at(n + 1, lambda: gather(i))
+                at(n, "post", lambda: gather(i))
             if kind == "w" and i == PASSES - 1:
                 stage_experts(n, u, v)
 
         waiting = []
-        n = 0
-        while n < len(steps) or waiting or any(k >= n for k in due):
+        for n in range(len(steps) + 9):
             if waiting and (len(waiting) == LAG or n >= len(steps)):
                 step, grouped = waiting.pop(0)
                 quantise(step, grouped)
                 after_quantise(n, step)
+            run(n, "first")
+            run(n, "pre")
             if n < len(steps):
                 issue_to(steps[n][0] + RAW_BUFS)
-                waiting.append((steps[n], interleave(steps[n])))
-            for fn in due.get(n, []):
-                fn()
-            n += 1
+                waiting.append((steps[n], interleave(steps[n], share(n))))
+            run(n, "post")
+            run(n, "late")

@@ -11,6 +11,7 @@ FP8X4 = mybir.dt.float8_e4m3fn_x4
 COPY = mybir.ActivationFunctionType.Copy
 RELU = mybir.ActivationFunctionType.Relu
 MULT = mybir.AluOpType.mult
+ADD = mybir.AluOpType.add
 
 P = 128
 K, T, E, C, N, M = 1024, 768, 4, 128, 1024, 512
@@ -21,18 +22,32 @@ SLOTS = E * C
 FLOPS = 2 * SLOTS * K * N + 2 * SLOTS * N * M
 BYTES = 4 * (K * T + E * K * N + N * E + N * M + SLOTS + M * T) + 2 * P * (SLOTS // 16)
 
-RAW_BUFS = 10
-LAG = 1
-ZL = (1, "post")
-SC = ((1, "late"), (2, "late"), (3, "late"), (4, "late"))
-S_EARLY, S_MID, S_LAST = 64, 88, 56
+Y_TIE = 1
+Z_TIE = 0
+ORDER = 1
+PAIRQ = 0
+MERGE = 0
+GB = 3
+RAW_BUFS = 12
+YL = 1
+ZL = 1
+PL = 1
+PMIN = 13
+TL = 0
+CL = 1
+SC = (1, 2, 3, 4)
+N_EARLY = 8
+S_EARLY, S_LAST = 48, 64
+S_PAT = (128, 32, 128, 16)
+G_PAT = (0, 0)
+G_PIECE = 128
 
 
 def tile_moe_nxt_lin_relu_kernel(tc, xT, w, b, wp, gate, offs, out):
     nc = tc.nc
     with ExitStack() as ctx:
         keep = ctx.enter_context(tc.tile_pool(name="keep", bufs=1))
-        rawp = ctx.enter_context(tc.tile_pool(name="rawp", bufs=RAW_BUFS))
+        rawp = ctx.enter_context(tc.tile_pool(name="rawp", bufs=1))
         stage = ctx.enter_context(tc.tile_pool(name="stage", bufs=4))
         psum = ctx.enter_context(tc.psum_pool(name="psum", bufs=3))
 
@@ -43,14 +58,13 @@ def tile_moe_nxt_lin_relu_kernel(tc, xT, w, b, wp, gate, offs, out):
         gates = keep.tile([P, SLOTS], F32, name="gates")
 
         x_codes = [keep.tile([P, T], U32, name=f"x_codes{i}", align_bytes=64) for i in range(PASSES)]
-        x_scales = [keep.tile([P, T], U8, name=f"x_scales{i}", align_bytes=64) for i in range(PASSES)]
+        x_scales = keep.tile([P, T], U8, name="x_scales", align_bytes=64)
         g_codes = [keep.tile([P, SLOTS], U32, name=f"g_codes{i}", align_bytes=64) for i in range(PASSES)]
-        g_scales = [keep.tile([P, SLOTS], U8, name=f"g_scales{i}", align_bytes=64) for i in range(PASSES)]
+        g_scales = keep.tile([P, SLOTS], U8, name="g_scales", align_bytes=64)
         wp_codes = [keep.tile([P, M], U32, name=f"wp_codes{i}", align_bytes=64) for i in range(PASSES)]
         wp_scales = [keep.tile([P, M], U8, name=f"wp_scales{i}", align_bytes=64) for i in range(PASSES)]
         outs = [keep.tile([P, T], F32, name=f"outs{i}") for i in range(M // P)]
-        for t in x_scales:
-            nc.gpsimd.memset(t[:], 0)
+        nc.gpsimd.memset(x_scales[:], 0)
         for t in outs:
             nc.gpsimd.memset(t[:], 0.0)
 
@@ -59,9 +73,14 @@ def tile_moe_nxt_lin_relu_kernel(tc, xT, w, b, wp, gate, offs, out):
 
         loads = []
 
+        def raw_tile(i, width):
+            return rawp.tile([P, 4, width], F32, name=f"raw{i % RAW_BUFS}")
+
         def load(src, width):
+            index = len(loads)
+
             def go():
-                raw = rawp.tile([P, 4, width], F32, name="raw")
+                raw = raw_tile(index, width)
                 nc.sync.dma_start(raw[:], src.rearrange("(p j) c -> p j c", j=4))
                 return raw
             loads.append(go)
@@ -76,10 +95,16 @@ def tile_moe_nxt_lin_relu_kernel(tc, xT, w, b, wp, gate, offs, out):
             for c0, c1 in ((0, 256), (256, 768)) if i == 0 else ((0, 512), (512, 768)):
                 steps.append((load(xT[i * PASS:(i + 1) * PASS, c0:c1], c1 - c0), 0, "x", i, c0, c1 - c0))
         small_after = len(loads)
-        for i in range(PASSES):
-            l = load(wp[i * PASS:(i + 1) * PASS, :], M)
-            steps.append((l, 0, "wp", i, 0, M))
+        def load_wp():
+            for i in range(PASSES):
+                l = load(wp[i * PASS:(i + 1) * PASS, :], M)
+                steps.append((l, 0, "wp", i, 0, M))
+
+        if ORDER == 0:
+            load_wp()
         for e in range(E):
+            if ORDER == 1 and e == 1:
+                load_wp()
             for a in range(2):
                 for i in range(PASSES):
                     l = load(w[e, i * PASS:(i + 1) * PASS, a * PASS:(a + 1) * PASS], PASS)
@@ -95,22 +120,34 @@ def tile_moe_nxt_lin_relu_kernel(tc, xT, w, b, wp, gate, offs, out):
                 raws[issued[0]] = loads[issued[0]]()
                 issued[0] += 1
 
-        def split_copy(dst, src, groups, sc):
+        def split_copy(dst, src, groups, sc, gc=0):
             cut = groups * sc // 128 // 4 * 4
-            nc.scalar.activation(dst[:, :cut], src[:, :cut], COPY)
-            nc.vector.tensor_copy(dst[:, cut:], src[:, cut:])
+            end = groups - groups * gc // 128 // 4 * 4
+            if cut:
+                nc.scalar.activation(dst[:, :cut], src[:, :cut], COPY)
+            if cut < end:
+                nc.vector.tensor_copy(dst[:, cut:end], src[:, cut:end])
+            g0 = end
+            while g0 < groups:
+                g1 = min(groups, g0 + G_PIECE)
+                nc.gpsimd.tensor_scalar(dst[:, g0:g1], src[:, g0:g1], 1.0, 0.0, MULT, ADD)
+                g0 = g1
 
         def share(n):
-            return S_EARLY if n < 10 else S_LAST if n >= len(steps) - 1 else S_MID
+            return S_EARLY if n < N_EARLY else S_LAST if n >= len(steps) - 1 else S_PAT[(n - 6) % len(S_PAT)]
+
+        pairs = {}
 
         def interleave(step, sc):
             l, c0, kind, i, u, v = step
             raw = raws[l]
             if kind == "w":
-                grouped = stage.tile([P, 2048], BF16, name="grouped_w", align_bytes=64)
-                dst = grouped[:].rearrange("p (r m j) -> p m j r", r=4, j=4)
+                if i == 0:
+                    pairs[u, v] = stage.tile([P, PASSES, 2048], BF16, name="grouped_w", align_bytes=64, bufs=GB)
+                grouped = pairs[u, v]
+                dst = grouped[:, i, :].rearrange("p (r m j) -> p m j r", r=4, j=4)
                 src = raw[:, :, c0:c0 + PASS].rearrange("p j (m r) -> p m j r", r=4)
-                split_copy(dst, src, 128, sc)
+                split_copy(dst, src, 128, sc, 0 if (u, v) == (E - 1, 1) else G_PAT[(2 * v + i) % len(G_PAT)])
             else:
                 width = v
                 grouped = stage.tile([P, 4 * width], BF16, name="grouped_x", align_bytes=64)
@@ -122,19 +159,25 @@ def tile_moe_nxt_lin_relu_kernel(tc, xT, w, b, wp, gate, offs, out):
         def quantise(step, grouped):
             l, c0, kind, i, u, v = step
             if kind == "x":
-                codes, scales = x_codes[i][:, u:u + v], x_scales[i][:, u:u + v]
+                nc.vector.quantize_mx(out=x_codes[i][:, u:u + v].bitcast(FP8X4), scales=x_scales[4 * i:P, u:u + v], in_=grouped[:])
             elif kind == "wp":
-                codes, scales = wp_codes[i][:], wp_scales[i][:]
+                nc.vector.quantize_mx(out=wp_codes[i][:].bitcast(FP8X4), scales=wp_scales[i][:], in_=grouped[:])
             else:
-                ct = keep.tile([P, PASS], U32, name=f"w_codes_{u}_{i}_{v}", align_bytes=64)
-                st = keep.tile([P, PASS], U8, name=f"w_scales_{u}_{i}_{v}", align_bytes=64)
-                w_codes[u, i, v], w_scales[u, i, v] = ct, st
-                codes, scales = ct[:], st[:]
-            nc.vector.quantize_mx(out=codes.bitcast(FP8X4), scales=scales, in_=grouped[:])
+                if i == 0:
+                    w_codes[u, v] = stage.tile([P, PASSES, PASS], U32, name="w_codes", align_bytes=64)
+                    w_scales[u, v] = stage.tile([P, PASSES, PASS], U8, name="w_scales", align_bytes=64)
+                codes, scales = w_codes[u, v], w_scales[u, v]
+                if (u, v) == (E - 1, 1) or not PAIRQ:
+                    nc.vector.quantize_mx(out=codes[:, i, :].bitcast(FP8X4), scales=scales[:, i, :], in_=grouped[:, i, :])
+                elif i == PASSES - 1:
+                    nc.vector.quantize_mx(
+                        out=codes[:].rearrange("p i c -> p (i c)").bitcast(FP8X4),
+                        scales=scales[:].rearrange("p i c -> p (i c)"), in_=grouped[:].rearrange("p i c -> p (i c)"))
 
         def gather(i):
             nc.vector.tensor_copy(g_codes[i][:], x_codes[i][:].indirect(offsets[:]))
-            nc.vector.tensor_copy(g_scales[i][:], x_scales[i][:].indirect(offsets[:]))
+            if i == PASSES - 1:
+                nc.vector.tensor_copy(g_scales[:], x_scales[:].indirect(offsets[:]))
 
         def experts(e, a):
             cols = slice(e * C, (e + 1) * C)
@@ -144,14 +187,22 @@ def tile_moe_nxt_lin_relu_kernel(tc, xT, w, b, wp, gate, offs, out):
                 for i in range(PASSES):
                     nc.tensor.matmul_mx(
                         out=acc[:, r, :],
-                        lhsT=w_codes[e, i, a][:, rows].bitcast(FP8X4), lhsT_scale=w_scales[e, i, a][:, rows],
-                        rhs=g_codes[i][:, cols].bitcast(FP8X4), rhs_scale=g_scales[i][:, cols],
+                        lhsT=w_codes[e, a][:, i, rows].bitcast(FP8X4), lhsT_scale=w_scales[e, a][:, i, rows],
+                        rhs=g_codes[i][:, cols].bitcast(FP8X4), rhs_scale=g_scales[4 * i:P, cols],
                         start=(i == 0), stop=(i == PASSES - 1),
                     )
             return acc
 
-        def activate(e, a, acc):
-            y = stage.tile([P, 4, C], F32, name="y")
+        ys = {}
+
+        def activate(n, e, a, acc):
+            if MERGE and e < E - 1:
+                if a == 0:
+                    ys[e] = rawp.tile([P, 2, 4, C], F32, name=f"raw{n % RAW_BUFS}")
+                y = ys[e][:, a, :, :]
+            else:
+                yt = raw_tile(n, C) if Y_TIE and n < len(steps) else stage.tile([P, 4, C], F32, name="y_end")
+                y = yt[:]
             for r in range(4):
                 nc.scalar.activation(y[:, r, :], acc[:, r, :], RELU, bias=bias[:, a, 4 * r + e:4 * r + e + 1])
             return y
@@ -159,14 +210,27 @@ def tile_moe_nxt_lin_relu_kernel(tc, xT, w, b, wp, gate, offs, out):
         def weigh(e, y):
             c = stage.tile([P, C, 4], BF16, name="c", align_bytes=64)
             g = gates[:, e * C:(e + 1) * C].unsqueeze(2).to_broadcast([P, C, 4])
-            nc.vector.tensor_tensor(c[:], y[:].rearrange("p r s -> p s r"), g, MULT)
+            nc.vector.tensor_tensor(c[:], y.rearrange("p r s -> p s r"), g, MULT)
             return c
+
+        def weigh_both(e):
+            c = stage.tile([P, 2, C, 4], BF16, name="c2", align_bytes=64)
+            g = gates[:, e * C:(e + 1) * C].unsqueeze(1).unsqueeze(3).to_broadcast([P, 2, C, 4])
+            nc.vector.tensor_tensor(c[:], ys[e][:].rearrange("p a r s -> p a s r"), g, MULT)
+            return c
+
+        def quantise_both(e, c):
+            codes = stage.tile([P, 2, C], U32, name="c_codes2", align_bytes=64)
+            scales = stage.tile([P, 2, C], U8, name="c_scales2", align_bytes=64)
+            nc.vector.quantize_mx(out=codes[:].rearrange("p a s -> p (a s)").bitcast(FP8X4), scales=scales[:].rearrange("p a s -> p (a s)"), in_=c[:].rearrange("p a s r -> p (a s r)"))
+            for a in range(2):
+                halves[e, a] = (codes[:, a, :], scales[:, a, :])
 
         def quantise_c(c):
             codes = stage.tile([P, C], U32, name="c_codes", align_bytes=64)
             scales = stage.tile([P, C], U8, name="c_scales", align_bytes=64)
             nc.vector.quantize_mx(out=codes[:].bitcast(FP8X4), scales=scales[:], in_=c[:].rearrange("p s r -> p (s r)"))
-            return codes, scales
+            return codes[:], scales[:]
 
         def project(halves):
             acc = psum.tile([P, 4, C], F32, name="acc_z")
@@ -177,13 +241,13 @@ def tile_moe_nxt_lin_relu_kernel(tc, xT, w, b, wp, gate, offs, out):
                     nc.tensor.matmul_mx(
                         out=acc[:, f, :],
                         lhsT=wp_codes[a][:, rows].bitcast(FP8X4), lhsT_scale=wp_scales[a][:, rows],
-                        rhs=codes[:].bitcast(FP8X4), rhs_scale=scales[:],
+                        rhs=codes.bitcast(FP8X4), rhs_scale=scales,
                         start=(a == 0), stop=(a == 1),
                     )
             return acc
 
-        def fetch(acc):
-            z = stage.tile([P, 4, C], F32, name="z")
+        def fetch(n, acc):
+            z = raw_tile(n, C) if Z_TIE and n < len(steps) else stage.tile([P, 4, C], F32, name="z_end")
             nc.scalar.activation(z[:], acc[:], COPY)
             return z
 
@@ -194,55 +258,64 @@ def tile_moe_nxt_lin_relu_kernel(tc, xT, w, b, wp, gate, offs, out):
 
         due = {}
 
-        def at(n, where, fn):
-            due.setdefault((n, where), []).append(fn)
+        def at(n, fn):
+            due.setdefault(n, []).append(fn)
 
-        def run(n, where):
-            for fn in due.get((n, where), []):
+        def run(n):
+            for fn in due.get(n, []):
                 fn()
 
         halves = {}
 
         def stage_experts(n, e, a):
             acc = experts(e, a)
-            at(n, "post", lambda: stage_activate(n, e, a, acc))
+            m = n - 1
+            at(m + YL, lambda: stage_activate(m + YL, e, a, acc))
 
         def stage_activate(n, e, a, acc):
-            y = activate(e, a, acc)
-            at(n + 1, "pre", lambda: stage_weigh(n + 1, e, a, y))
+            y = activate(n, e, a, acc)
+            at(n + TL, lambda: stage_weigh(n + TL, e, a, y))
 
         def stage_weigh(n, e, a, y):
-            c = weigh(e, y)
-            at(n, "post", lambda: stage_c(n, e, a, c))
+            if MERGE and e < E - 1:
+                if a == 0:
+                    return
+                c = weigh_both(e)
+            else:
+                c = weigh(e, y)
+            at(n + CL, lambda: stage_c(n + CL, e, a, c))
 
         def stage_c(n, e, a, c):
-            halves[e, a] = quantise_c(c)
+            if MERGE and e < E - 1:
+                quantise_both(e, c)
+            else:
+                halves[e, a] = quantise_c(c)
             if a == 1:
-                acc = project([halves[e, 0], halves[e, 1]])
-                at(n + ZL[0], ZL[1], lambda: stage_fetch(n + ZL[0], e, acc))
+                at(max(n + PL, PMIN), lambda: stage_project(max(n + PL, PMIN), e))
+
+        def stage_project(n, e):
+            acc = project([halves[e, 0], halves[e, 1]])
+            at(n + ZL, lambda: stage_fetch(n + ZL, e, acc))
 
         def stage_fetch(n, e, acc):
-            z = fetch(acc)
+            z = fetch(n, acc)
             for f in range(M // P):
-                at(n + SC[f][0], SC[f][1], lambda f=f: scatter(e, z, f))
+                at(n + SC[f], lambda f=f: scatter(e, z, f))
 
         def after_quantise(n, step):
             l, c0, kind, i, u, v = step
             if kind == "x" and u + v == T:
-                at(n, "post", lambda: gather(i))
+                at(n, lambda: gather(i))
             if kind == "w" and i == PASSES - 1:
                 stage_experts(n, u, v)
 
-        waiting = []
-        for n in range(len(steps) + 9):
-            if waiting and (len(waiting) == LAG or n >= len(steps)):
-                step, grouped = waiting.pop(0)
-                quantise(step, grouped)
-                after_quantise(n, step)
-            run(n, "first")
-            run(n, "pre")
+        waiting = None
+        for n in range(len(steps) + 20):
             if n < len(steps):
-                issue_to(steps[n][0] + RAW_BUFS)
-                waiting.append((steps[n], interleave(steps[n], share(n))))
-            run(n, "post")
-            run(n, "late")
+                issue_to(n + RAW_BUFS)
+                grouped = interleave(steps[n], share(n))
+            if waiting:
+                quantise(*waiting)
+                after_quantise(n, waiting[0])
+            waiting = (steps[n], grouped) if n < len(steps) else None
+            run(n)

@@ -26,8 +26,8 @@ Y_TIE = 1
 Z_TIE = 0
 ORDER = 1
 PAIRQ = 0
-MERGE = 0
-GB = 3
+MERGE = 1
+GB = 4
 RAW_BUFS = 12
 YL = 1
 ZL = 1
@@ -35,12 +35,10 @@ PL = 1
 PMIN = 13
 TL = 0
 CL = 1
-SC = (1, 2, 3, 4)
-N_EARLY = 8
-S_EARLY, S_LAST = 48, 64
-S_PAT = (128, 32, 128, 16)
-G_PAT = (0, 0)
-G_PIECE = 128
+SC = (0, 1, 2, 3)
+N_EARLY = 14
+S_EARLY, S_LAST = 48, 80
+S_PAT = (128, 0)
 
 
 def tile_moe_nxt_lin_relu_kernel(tc, xT, w, b, wp, gate, offs, out):
@@ -120,18 +118,16 @@ def tile_moe_nxt_lin_relu_kernel(tc, xT, w, b, wp, gate, offs, out):
                 raws[issued[0]] = loads[issued[0]]()
                 issued[0] += 1
 
-        def split_copy(dst, src, groups, sc, gc=0):
+        def split_copy(dst, src, groups, sc, pairwise=False):
             cut = groups * sc // 128 // 4 * 4
-            end = groups - groups * gc // 128 // 4 * 4
+            end = groups
             if cut:
                 nc.scalar.activation(dst[:, :cut], src[:, :cut], COPY)
-            if cut < end:
+            if cut < end and pairwise:
+                for h in range(2):
+                    nc.vector.tensor_copy(dst[:, cut:end, :, 2 * h:2 * h + 2], src[:, cut:end, :, 2 * h:2 * h + 2])
+            elif cut < end:
                 nc.vector.tensor_copy(dst[:, cut:end], src[:, cut:end])
-            g0 = end
-            while g0 < groups:
-                g1 = min(groups, g0 + G_PIECE)
-                nc.gpsimd.tensor_scalar(dst[:, g0:g1], src[:, g0:g1], 1.0, 0.0, MULT, ADD)
-                g0 = g1
 
         def share(n):
             return S_EARLY if n < N_EARLY else S_LAST if n >= len(steps) - 1 else S_PAT[(n - 6) % len(S_PAT)]
@@ -147,7 +143,7 @@ def tile_moe_nxt_lin_relu_kernel(tc, xT, w, b, wp, gate, offs, out):
                 grouped = pairs[u, v]
                 dst = grouped[:, i, :].rearrange("p (r m j) -> p m j r", r=4, j=4)
                 src = raw[:, :, c0:c0 + PASS].rearrange("p j (m r) -> p m j r", r=4)
-                split_copy(dst, src, 128, sc, 0 if (u, v) == (E - 1, 1) else G_PAT[(2 * v + i) % len(G_PAT)])
+                split_copy(dst, src, 128, sc, True)
             else:
                 width = v
                 grouped = stage.tile([P, 4 * width], BF16, name="grouped_x", align_bytes=64)
@@ -207,16 +203,23 @@ def tile_moe_nxt_lin_relu_kernel(tc, xT, w, b, wp, gate, offs, out):
                 nc.scalar.activation(y[:, r, :], acc[:, r, :], RELU, bias=bias[:, a, 4 * r + e:4 * r + e + 1])
             return y
 
+        def weigh_into(c, e, y):
+            nc.vector.tensor_tensor(
+                c.rearrange("p (u v) r -> p u r v", v=2),
+                y.rearrange("p r (u v) -> p u r v", v=2),
+                gates[:, e * C:(e + 1) * C].rearrange("p (u v) -> p u v", v=2).unsqueeze(2).to_broadcast([P, C // 2, 4, 2]),
+                MULT,
+            )
+
         def weigh(e, y):
             c = stage.tile([P, C, 4], BF16, name="c", align_bytes=64)
-            g = gates[:, e * C:(e + 1) * C].unsqueeze(2).to_broadcast([P, C, 4])
-            nc.vector.tensor_tensor(c[:], y.rearrange("p r s -> p s r"), g, MULT)
+            weigh_into(c[:], e, y)
             return c
 
         def weigh_both(e):
             c = stage.tile([P, 2, C, 4], BF16, name="c2", align_bytes=64)
-            g = gates[:, e * C:(e + 1) * C].unsqueeze(1).unsqueeze(3).to_broadcast([P, 2, C, 4])
-            nc.vector.tensor_tensor(c[:], ys[e][:].rearrange("p a r s -> p a s r"), g, MULT)
+            for a in range(2):
+                weigh_into(c[:, a, :, :], e, ys[e][:, a, :, :])
             return c
 
         def quantise_both(e, c):

@@ -23,22 +23,23 @@ FLOPS = 2 * SLOTS * K * N + 2 * SLOTS * N * M
 BYTES = 4 * (K * T + E * K * N + N * E + N * M + SLOTS + M * T) + 2 * P * (SLOTS // 16)
 
 Y_TIE = 1
-Z_TIE = 0
+Z_TIE = 1
 ORDER = 1
 PAIRQ = 0
+ZSPLIT = 1
 MERGE = 1
-GB = 4
-RAW_BUFS = 12
+GB = 3
+RAW_BUFS = 11
 YL = 1
-ZL = 1
-PL = 1
+ZL = 0
+PL = 0
 PMIN = 13
-TL = 0
+TL = 1
 CL = 1
 SC = (0, 1, 2, 3)
 N_EARLY = 14
-S_EARLY, S_LAST = 48, 80
-S_PAT = (128, 0)
+S_EARLY, S_LAST = 64, 48
+S_PAT = (128, 24)
 
 
 def tile_moe_nxt_lin_relu_kernel(tc, xT, w, b, wp, gate, offs, out):
@@ -249,9 +250,13 @@ def tile_moe_nxt_lin_relu_kernel(tc, xT, w, b, wp, gate, offs, out):
                     )
             return acc
 
-        def fetch(n, acc):
+        def fetch(n, e, acc):
             z = raw_tile(n, C) if Z_TIE and n < len(steps) else stage.tile([P, 4, C], F32, name="z_end")
-            nc.scalar.activation(z[:], acc[:], COPY)
+            if e == E - 1 and ZSPLIT:
+                for f in range(M // P):
+                    nc.scalar.activation(z[:, f, :], acc[:, f, :], COPY)
+            else:
+                nc.scalar.activation(z[:], acc[:], COPY)
             return z
 
         def scatter(e, z, f):
@@ -301,7 +306,7 @@ def tile_moe_nxt_lin_relu_kernel(tc, xT, w, b, wp, gate, offs, out):
             at(n + ZL, lambda: stage_fetch(n + ZL, e, acc))
 
         def stage_fetch(n, e, acc):
-            z = fetch(n, acc)
+            z = fetch(n, e, acc)
             for f in range(M // P):
                 at(n + SC[f], lambda f=f: scatter(e, z, f))
 

from contextlib import ExitStack

import concourse.mybir as mybir

F32 = mybir.dt.float32
BF16 = mybir.dt.bfloat16
U32 = mybir.dt.uint32
U16 = mybir.dt.uint16
U8 = mybir.dt.uint8
FP8X4 = mybir.dt.float8_e4m3fn_x4
COPY = mybir.ActivationFunctionType.Copy
RELU = mybir.ActivationFunctionType.Relu
MULT = mybir.AluOpType.mult
ADD = mybir.AluOpType.add

P = 128
K, T, E, C, N, M = 1024, 768, 4, 128, 1024, 512
PASS = 512
PASSES = K // PASS
SLOTS = E * C

FLOPS = 2 * SLOTS * K * N + 2 * SLOTS * N * M
BYTES = 4 * (K * T + E * K * N + N * E + N * M + SLOTS + M * T) + 2 * P * (SLOTS // 16)

Y_TIE = 1
Z_TIE = 1
ORDER = 1
PAIRQ = 0
ZSPLIT = 1
MERGE = 1
GB = 3
RAW_BUFS = 11
YL = 1
ZL = 0
PL = 0
PMIN = 13
TL = 1
CL = 1
SC = (0, 1, 2, 3)
N_EARLY = 14
S_EARLY, S_LAST = 64, 48
S_PAT = (128, 24)


def tile_moe_nxt_lin_relu_kernel(tc, xT, w, b, wp, gate, offs, out):
    nc = tc.nc
    with ExitStack() as ctx:
        keep = ctx.enter_context(tc.tile_pool(name="keep", bufs=1))
        rawp = ctx.enter_context(tc.tile_pool(name="rawp", bufs=1))
        stage = ctx.enter_context(tc.tile_pool(name="stage", bufs=4))
        psum = ctx.enter_context(tc.psum_pool(name="psum", bufs=3))

        offsets = keep.tile([P, SLOTS // 16], U16, name="offsets")
        nc.sync.dma_start(offsets[:], offs)

        bias = keep.tile([P, 2, 16], F32, name="bias")
        gates = keep.tile([P, SLOTS], F32, name="gates")

        x_codes = [keep.tile([P, T], U32, name=f"x_codes{i}", align_bytes=64) for i in range(PASSES)]
        x_scales = keep.tile([P, T], U8, name="x_scales", align_bytes=64)
        g_codes = [keep.tile([P, SLOTS], U32, name=f"g_codes{i}", align_bytes=64) for i in range(PASSES)]
        g_scales = keep.tile([P, SLOTS], U8, name="g_scales", align_bytes=64)
        wp_codes = [keep.tile([P, M], U32, name=f"wp_codes{i}", align_bytes=64) for i in range(PASSES)]
        wp_scales = [keep.tile([P, M], U8, name=f"wp_scales{i}", align_bytes=64) for i in range(PASSES)]
        outs = [keep.tile([P, T], F32, name=f"outs{i}") for i in range(M // P)]
        nc.gpsimd.memset(x_scales[:], 0)
        for t in outs:
            nc.gpsimd.memset(t[:], 0.0)

        w_codes = {}
        w_scales = {}

        loads = []

        def raw_tile(i, width):
            return rawp.tile([P, 4, width], F32, name=f"raw{i % RAW_BUFS}")

        def load(src, width):
            index = len(loads)

            def go():
                raw = raw_tile(index, width)
                nc.sync.dma_start(raw[:], src.rearrange("(p j) c -> p j c", j=4))
                return raw
            loads.append(go)
            return len(loads) - 1

        def load_small():
            nc.sync.dma_start(gates[:], gate[0:P, :])
            nc.sync.dma_start(bias[:].rearrange("p a (r e) -> p a r e", r=4), b.rearrange("(a q r) e -> q a r e", a=2, r=4))

        steps = []
        for i in range(PASSES):
            for c0, c1 in ((0, 256), (256, 768)) if i == 0 else ((0, 512), (512, 768)):
                steps.append((load(xT[i * PASS:(i + 1) * PASS, c0:c1], c1 - c0), 0, "x", i, c0, c1 - c0))
        small_after = len(loads)
        def load_wp():
            for i in range(PASSES):
                l = load(wp[i * PASS:(i + 1) * PASS, :], M)
                steps.append((l, 0, "wp", i, 0, M))

        if ORDER == 0:
            load_wp()
        for e in range(E):
            if ORDER == 1 and e == 1:
                load_wp()
            for a in range(2):
                for i in range(PASSES):
                    l = load(w[e, i * PASS:(i + 1) * PASS, a * PASS:(a + 1) * PASS], PASS)
                    steps.append((l, 0, "w", i, e, a))

        raws = {}
        issued = [0]

        def issue_to(n):
            while issued[0] < min(n, len(loads)):
                if issued[0] == small_after:
                    load_small()
                raws[issued[0]] = loads[issued[0]]()
                issued[0] += 1

        def split_copy(dst, src, groups, sc, pairwise=False):
            cut = groups * sc // 128 // 4 * 4
            end = groups
            if cut:
                nc.scalar.activation(dst[:, :cut], src[:, :cut], COPY)
            if cut < end and pairwise:
                for h in range(2):
                    nc.vector.tensor_copy(dst[:, cut:end, :, 2 * h:2 * h + 2], src[:, cut:end, :, 2 * h:2 * h + 2])
            elif cut < end:
                nc.vector.tensor_copy(dst[:, cut:end], src[:, cut:end])

        def share(n):
            return S_EARLY if n < N_EARLY else S_LAST if n >= len(steps) - 1 else S_PAT[(n - 6) % len(S_PAT)]

        pairs = {}

        def interleave(step, sc):
            l, c0, kind, i, u, v = step
            raw = raws[l]
            if kind == "w":
                if i == 0:
                    pairs[u, v] = stage.tile([P, PASSES, 2048], BF16, name="grouped_w", align_bytes=64, bufs=GB)
                grouped = pairs[u, v]
                dst = grouped[:, i, :].rearrange("p (r m j) -> p m j r", r=4, j=4)
                src = raw[:, :, c0:c0 + PASS].rearrange("p j (m r) -> p m j r", r=4)
                split_copy(dst, src, 128, sc, True)
            else:
                width = v
                grouped = stage.tile([P, 4 * width], BF16, name="grouped_x", align_bytes=64)
                dst = grouped[:].rearrange("p (g c j) -> p g j c", c=4, j=4)
                src = raw[:, :, :].rearrange("p j (g c) -> p g j c", c=4)
                split_copy(dst, src, width // 4, sc)
            return grouped

        def quantise(step, grouped):
            l, c0, kind, i, u, v = step
            if kind == "x":
                nc.vector.quantize_mx(out=x_codes[i][:, u:u + v].bitcast(FP8X4), scales=x_scales[4 * i:P, u:u + v], in_=grouped[:])
            elif kind == "wp":
                nc.vector.quantize_mx(out=wp_codes[i][:].bitcast(FP8X4), scales=wp_scales[i][:], in_=grouped[:])
            else:
                if i == 0:
                    w_codes[u, v] = stage.tile([P, PASSES, PASS], U32, name="w_codes", align_bytes=64)
                    w_scales[u, v] = stage.tile([P, PASSES, PASS], U8, name="w_scales", align_bytes=64)
                codes, scales = w_codes[u, v], w_scales[u, v]
                if (u, v) == (E - 1, 1) or not PAIRQ:
                    nc.vector.quantize_mx(out=codes[:, i, :].bitcast(FP8X4), scales=scales[:, i, :], in_=grouped[:, i, :])
                elif i == PASSES - 1:
                    nc.vector.quantize_mx(
                        out=codes[:].rearrange("p i c -> p (i c)").bitcast(FP8X4),
                        scales=scales[:].rearrange("p i c -> p (i c)"), in_=grouped[:].rearrange("p i c -> p (i c)"))

        def gather(i):
            nc.vector.tensor_copy(g_codes[i][:], x_codes[i][:].indirect(offsets[:]))
            if i == PASSES - 1:
                nc.vector.tensor_copy(g_scales[:], x_scales[:].indirect(offsets[:]))

        def experts(e, a):
            cols = slice(e * C, (e + 1) * C)
            acc = psum.tile([P, 4, C], F32, name="acc_y")
            for r in range(4):
                rows = slice(r * P, (r + 1) * P)
                for i in range(PASSES):
                    nc.tensor.matmul_mx(
                        out=acc[:, r, :],
                        lhsT=w_codes[e, a][:, i, rows].bitcast(FP8X4), lhsT_scale=w_scales[e, a][:, i, rows],
                        rhs=g_codes[i][:, cols].bitcast(FP8X4), rhs_scale=g_scales[4 * i:P, cols],
                        start=(i == 0), stop=(i == PASSES - 1),
                    )
            return acc

        ys = {}

        def activate(n, e, a, acc):
            if MERGE and e < E - 1:
                if a == 0:
                    ys[e] = rawp.tile([P, 2, 4, C], F32, name=f"raw{n % RAW_BUFS}")
                y = ys[e][:, a, :, :]
            else:
                yt = raw_tile(n, C) if Y_TIE and n < len(steps) else stage.tile([P, 4, C], F32, name="y_end")
                y = yt[:]
            for r in range(4):
                nc.scalar.activation(y[:, r, :], acc[:, r, :], RELU, bias=bias[:, a, 4 * r + e:4 * r + e + 1])
            return y

        def weigh_into(c, e, y):
            nc.vector.tensor_tensor(
                c.rearrange("p (u v) r -> p u r v", v=2),
                y.rearrange("p r (u v) -> p u r v", v=2),
                gates[:, e * C:(e + 1) * C].rearrange("p (u v) -> p u v", v=2).unsqueeze(2).to_broadcast([P, C // 2, 4, 2]),
                MULT,
            )

        def weigh(e, y):
            c = stage.tile([P, C, 4], BF16, name="c", align_bytes=64)
            weigh_into(c[:], e, y)
            return c

        def weigh_both(e):
            c = stage.tile([P, 2, C, 4], BF16, name="c2", align_bytes=64)
            for a in range(2):
                weigh_into(c[:, a, :, :], e, ys[e][:, a, :, :])
            return c

        def quantise_both(e, c):
            codes = stage.tile([P, 2, C], U32, name="c_codes2", align_bytes=64)
            scales = stage.tile([P, 2, C], U8, name="c_scales2", align_bytes=64)
            nc.vector.quantize_mx(out=codes[:].rearrange("p a s -> p (a s)").bitcast(FP8X4), scales=scales[:].rearrange("p a s -> p (a s)"), in_=c[:].rearrange("p a s r -> p (a s r)"))
            for a in range(2):
                halves[e, a] = (codes[:, a, :], scales[:, a, :])

        def quantise_c(c):
            codes = stage.tile([P, C], U32, name="c_codes", align_bytes=64)
            scales = stage.tile([P, C], U8, name="c_scales", align_bytes=64)
            nc.vector.quantize_mx(out=codes[:].bitcast(FP8X4), scales=scales[:], in_=c[:].rearrange("p s r -> p (s r)"))
            return codes[:], scales[:]

        def project(halves):
            acc = psum.tile([P, 4, C], F32, name="acc_z")
            for f in range(M // P):
                rows = slice(f * P, (f + 1) * P)
                for a in range(2):
                    codes, scales = halves[a]
                    nc.tensor.matmul_mx(
                        out=acc[:, f, :],
                        lhsT=wp_codes[a][:, rows].bitcast(FP8X4), lhsT_scale=wp_scales[a][:, rows],
                        rhs=codes.bitcast(FP8X4), rhs_scale=scales,
                        start=(a == 0), stop=(a == 1),
                    )
            return acc

        def fetch(n, e, acc):
            z = raw_tile(n, C) if Z_TIE and n < len(steps) else stage.tile([P, 4, C], F32, name="z_end")
            if e == E - 1 and ZSPLIT:
                for f in range(M // P):
                    nc.scalar.activation(z[:, f, :], acc[:, f, :], COPY)
            else:
                nc.scalar.activation(z[:], acc[:], COPY)
            return z

        def scatter(e, z, f):
            nc.vector.tensor_copy(outs[f][:].indirect(offsets[:, e * (C // 16):(e + 1) * (C // 16)]), z[:, f, :])
            if e == E - 1:
                nc.sync.dma_start(out[f * P:(f + 1) * P, :], outs[f][:])

        due = {}

        def at(n, fn):
            due.setdefault(n, []).append(fn)

        def run(n):
            for fn in due.get(n, []):
                fn()

        halves = {}

        def stage_experts(n, e, a):
            acc = experts(e, a)
            m = n - 1
            at(m + YL, lambda: stage_activate(m + YL, e, a, acc))

        def stage_activate(n, e, a, acc):
            y = activate(n, e, a, acc)
            at(n + TL, lambda: stage_weigh(n + TL, e, a, y))

        def stage_weigh(n, e, a, y):
            if MERGE and e < E - 1:
                if a == 0:
                    return
                c = weigh_both(e)
            else:
                c = weigh(e, y)
            at(n + CL, lambda: stage_c(n + CL, e, a, c))

        def stage_c(n, e, a, c):
            if MERGE and e < E - 1:
                quantise_both(e, c)
            else:
                halves[e, a] = quantise_c(c)
            if a == 1:
                at(max(n + PL, PMIN), lambda: stage_project(max(n + PL, PMIN), e))

        def stage_project(n, e):
            acc = project([halves[e, 0], halves[e, 1]])
            at(n + ZL, lambda: stage_fetch(n + ZL, e, acc))

        def stage_fetch(n, e, acc):
            z = fetch(n, e, acc)
            for f in range(M // P):
                at(n + SC[f], lambda f=f: scatter(e, z, f))

        def after_quantise(n, step):
            l, c0, kind, i, u, v = step
            if kind == "x" and u + v == T:
                at(n, lambda: gather(i))
            if kind == "w" and i == PASSES - 1:
                stage_experts(n, u, v)

        waiting = None
        for n in range(len(steps) + 20):
            if n < len(steps):
                issue_to(n + RAW_BUFS)
                grouped = interleave(steps[n], share(n))
            if waiting:
                quantise(*waiting)
                after_quantise(n, waiting[0])
            waiting = (steps[n], grouped) if n < len(steps) else None
            run(n)
